import numpy as np
import ml_dtypes


def mxq(x, axis, fmt="e4m3"):
    dtype, down = {"e4m3": (ml_dtypes.float8_e4m3fn, 7), "e5m2": (ml_dtypes.float8_e5m2, 14)}[fmt]
    v = np.moveaxis(np.asarray(x, np.float32).astype(ml_dtypes.bfloat16).astype(np.float64), axis, -1)
    blocks = v.reshape(v.shape[:-1] + (-1, 32))
    amax = np.abs(blocks).max(-1, keepdims=True)
    byte = np.maximum(np.where(amax > 0, np.frexp(amax)[1] - 1 + 127, 0) - down, 1)
    scale = np.exp2(byte - 127.0)
    codes = (blocks / scale).astype(np.float32).astype(dtype).astype(np.float64)
    return np.moveaxis((codes * scale).reshape(v.shape), -1, axis)


WIDE = False


def mx_kscale(k, group=512):
    if not WIDE:
        return np.ones(k)
    levels = np.array([18, -18])
    if group != 512:
        return np.exp2(np.random.permutation(np.resize(levels, k // group))).repeat(group)
    if k % 512:
        return np.exp2(np.random.permutation(np.resize(levels, k // 32))).repeat(32)
    a = np.empty((k // 512, 16))
    for p in range(k // 512):
        a[p, :8] = np.random.permutation(np.resize(levels, 8))
        for g in range(8):
            far = levels[np.abs(levels - a[p, g]) >= 10]
            a[p, g + 8] = far[np.random.randint(len(far))]
    return np.exp2(a.ravel()).repeat(32)


def f64(x):
    return np.asarray(x).astype(np.float64)


def gelu(v):
    return 0.5 * v * (1.0 + np.tanh(0.7978845608028654 * (v + 0.044715 * v ** 3)))


def bf(x):
    return np.asarray(x, np.float32).astype(ml_dtypes.bfloat16)


def planes(Y):
    r, m = Y.shape
    b = f64(bf(Y)).reshape(r // 32, 32, m)
    amax = np.abs(b).max(1)
    byte = np.clip(np.where(amax > 0, np.frexp(amax)[1] - 1 + 127 - 7, 1), 1, 254)
    codes = (b * np.exp2(127.0 - byte)[:, None, :]).reshape(r, m).astype(np.float32).astype(ml_dtypes.float8_e4m3fn).view(np.uint8)
    words = codes.reshape(r // 512, 128, 4, m).transpose(0, 1, 3, 2)
    return np.ascontiguousarray(words), np.ascontiguousarray(byte.astype(np.uint8).reshape(r // 512, 16, m))


G, D, J, K, L = 8, 128, 128, 128, 128


def sgn(shape):
    return np.random.uniform(0.5, 2.0, shape) * np.where(np.random.standard_normal(shape) < 0, -1.0, 1.0)


def setup_inputs():
    n = np.random.standard_normal
    s_d = mx_kscale(D, 0)
    s_j = mx_kscale(J, 0)
    return {
        "x": (n((G, D, J)) * s_d[:, None]).astype(np.float32),
        "a": (n((G, D, K)) / np.sqrt(D) / s_d[:, None]).astype(np.float32),
        "bj": (0.5 * n((G, J, 1))).astype(np.float32),
        "hs": (sgn((G, J, 1)) * s_j[:, None]).astype(np.float32),
        "b": (n((G, J, L)) / np.sqrt(J) / s_j[:, None]).astype(np.float32),
        "r": (n((G, K, L))).astype(np.float32),
    }


def reference(x, a, bj, hs, b, r):
    xq = mxq(f64(x), 1, "e4m3")
    aq = mxq(f64(a), 1, "e4m3")
    z = xq.transpose(0, 2, 1) @ aq
    h = gelu(z + f64(bj)) * f64(hs)
    hq = mxq(h, 1, "e4m3")
    bq = mxq(f64(b), 1, "e4m3")
    w = hq.transpose(0, 2, 1) @ bq
    y = w + f64(r)
    Y = y.reshape(G * K, L)
    words, scales = planes(Y)
    return Y, words, scales

@@ -1,0 +1,181 @@
+from contextlib import ExitStack
+
+import concourse.mybir as mybir
+
+G, D, J, K, L = 8, 128, 128, 128, 128
+FLOPS = 2 * G * D * J * K + 2 * G * J * K * L
+
+F32 = mybir.dt.float32
+BF16 = mybir.dt.bfloat16
+U32 = mybir.dt.uint32
+I32 = mybir.dt.int32
+U8 = mybir.dt.uint8
+FP8X4 = mybir.dt.float8_e4m3fn_x4
+ACT = mybir.ActivationFunctionType
+ALU = mybir.AluOpType
+
+P = 128
+PACK = 4
+ROWS = 32
+SIDE = 4
+SETS = 2
+W = 128
+RUN = 4
+
+
+def tile_rows_pl_kron_gelu_kernel(tc, x, a, bj, hs, b, r, out_0, out_1, out_2):
+    nc = tc.nc
+    with ExitStack() as ctx:
+        sb = ctx.enter_context(tc.tile_pool(name="sb", bufs=1))
+        ps = ctx.enter_context(tc.psum_pool(name="ps", bufs=1))
+        ctx.enter_context(tc.manual_schedule())
+
+        def new(name, shape, dtype):
+            return sb.tile(shape, dtype, name=name, align_bytes=64)
+
+        def packed_rows(t, s):
+            return t[SIDE * s : SIDE * (s + 1)].rearrange("c (p j) n -> (c p) j n", j=PACK)
+
+        def interleave(copy, dst, src):
+            copy(
+                out=dst.rearrange("p (c i) t -> p c t i", i=RUN),
+                in_=src.rearrange("p t (c i) -> p c t i", i=RUN),
+            )
+
+        def quantize(codes, scales, grouped):
+            nc.vector.quantize_mx(
+                out=codes.bitcast(FP8X4), scales=scales, in_=grouped.rearrange("p n t -> p (n t)")
+            )
+
+        def product(acc, c, lc, ls, rc, rs):
+            rows = slice(ROWS * c, ROWS * (c + 1))
+            nc.tensor.matmul_mx(
+                out=acc, lhsT=lc[rows, :].bitcast(FP8X4), lhsT_scale=ls[rows, :],
+                rhs=rc[rows, :].bitcast(FP8X4), rhs_scale=rs[rows, :], start=True, stop=True,
+            )
+
+        def operand(name):
+            raw_dt = BF16 if name[0] == "h" else F32
+            return {
+                "raw": new(name + "_raw", [P, PACK, W], raw_dt),
+                "grp": new(name + "_grp", [P, W, PACK], BF16),
+                "codes": new(name + "_codes", [P, W], U32),
+                "scales": new(name + "_scales", [P, W], U8),
+            }
+
+        xs = [operand("x%d" % s) for s in range(SETS)]
+        As = [operand("a%d" % s) for s in range(SETS)]
+        bs = [operand("b%d" % s) for s in range(SETS)]
+        hq = [operand("h%d" % s) for s in range(SETS)]
+        y_raw = [new("y_raw%d" % s, [P, PACK, W], F32) for s in range(SETS)]
+        y_grp = [new("y_grp%d" % s, [P, W, PACK], BF16) for s in range(SETS)]
+        y_codes = [new("y_codes%d" % s, [P, W], U32) for s in range(SETS)]
+        y_scales = new("y_scales", [P, SETS * W], U8)
+        r_sb = [new("r%d" % s, [P, SIDE, W], F32) for s in range(SETS)]
+        act = [new("act%d" % g, [P, W], F32) for g in range(G)]
+        h_nat = [new("h_nat%d" % g, [P, W], BF16) for g in range(G)]
+        y_nat = [new("y_nat%d" % g, [P, W], F32) for g in range(G)]
+        banks = [ps.tile([P, 512], F32, name="bank%d" % g) for g in range(G)]
+        vec_rows = new("vec_rows", [P, G * ROWS], F32)
+        vec_cols = new("vec_cols", [P, G * ROWS], F32)
+
+        def iq(op, copy=nc.vector.tensor_copy):
+            interleave(copy, op["grp"][:], op["raw"][:])
+
+        def q(op):
+            quantize(op["codes"][:], op["scales"][:], op["grp"][:])
+
+        def load_r(s):
+            nc.sync.dma_start(out=r_sb[s][:], in_=r[SIDE * s : SIDE * (s + 1)].rearrange("c k l -> k c l"))
+
+        nc.gpsimd.memset(vec_rows[:], 0.0)
+        for s in range(SETS):
+            nc.sync.dma_start(out=xs[s]["raw"][:], in_=packed_rows(x, s))
+            nc.sync.dma_start(out=As[s]["raw"][:], in_=packed_rows(a, s))
+        for row, v in enumerate((bj, hs)):
+            nc.scalar.dma_start(
+                out=vec_rows[row:P:ROWS, :].rearrange("q (g i) -> q g i", i=ROWS),
+                in_=v.rearrange("g (q i) o -> q g (i o)", i=ROWS),
+            )
+        for s in range(SETS):
+            nc.sync.dma_start(out=bs[s]["raw"][:], in_=packed_rows(b, s))
+
+        def first_products(s):
+            for c in range(SIDE):
+                product(banks[SIDE * s + c][:, 0:W], c, xs[s]["codes"], xs[s]["scales"], As[s]["codes"], As[s]["scales"])
+
+        def gelu(g):
+            nc.scalar.activation(out=act[g][:], in_=banks[g][:, 0:W], func=ACT.Gelu_apprx_tanh,
+                                 bias=vec_cols[:, ROWS * g : ROWS * g + 1])
+
+        def scale(g):
+            nc.vector.tensor_scalar(out=h_nat[g][:], in0=act[g][:], scalar1=vec_cols[:, ROWS * g + 1 : ROWS * g + 2],
+                                    scalar2=None, op0=ALU.mult)
+
+        def move(dst, src, g):
+            c = g % SIDE
+            nc.sync.dma_start(out=dst[ROWS * c : ROWS * (c + 1), :, :], in_=src[:])
+
+        def second_products(s):
+            for c in range(SIDE):
+                product(banks[SIDE * s + c][:, W : 2 * W], c, hq[s]["codes"], hq[s]["scales"], bs[s]["codes"], bs[s]["scales"])
+
+        def add(g):
+            nc.vector.tensor_tensor(out=y_nat[g][:], in0=banks[g][:, W : 2 * W], in1=r_sb[g // SIDE][:, g % SIDE, :], op=ALU.add)
+            move(y_raw[g // SIDE], y_nat[g], g)
+
+        iq(xs[0])
+        nc.vector.transpose(out=vec_cols[:], in_=vec_rows[:])
+        q(xs[0])
+        iq(As[0])
+        q(As[0])
+        first_products(0)
+        iq(xs[1])
+        q(xs[1])
+        iq(As[1])
+        q(As[1])
+        first_products(1)
+        load_r(0)
+        for g in range(4):
+            gelu(g)
+            scale(g)
+            move(hq[0]["raw"], h_nat[g], g)
+        iq(bs[0])
+        for g in range(4, 8):
+            gelu(g)
+            scale(g)
+            move(hq[1]["raw"], h_nat[g], g)
+        load_r(1)
+        iq(bs[1])
+        q(bs[0])
+        iq(hq[0])
+        q(bs[1])
+        q(hq[0])
+        second_products(0)
+        iq(hq[1])
+        add(0)
+        q(hq[1])
+        second_products(1)
+        for g in range(1, 8):
+            add(g)
+
+        def store_y(s, eng):
+            eng.dma_start(out=out_0[512 * s : 512 * (s + 1), :].rearrange("(p t) l -> p t l", t=PACK), in_=y_raw[s][:])
+
+        def store_words(s, eng):
+            eng.dma_start(out=out_1[s].rearrange("p l u -> p (l u)").bitcast(I32), in_=y_codes[s][:].bitcast(I32))
+
+        store_y(0, nc.scalar)
+        interleave(nc.vector.tensor_copy, y_grp[0][:], y_raw[0][:])
+        quantize(y_codes[0][:], y_scales[:, 0:W], y_grp[0][:])
+        store_words(0, nc.sync)
+        store_y(1, nc.scalar)
+        interleave(nc.vector.tensor_copy, y_grp[1][:], y_raw[1][:])
+        quantize(y_codes[1][:], y_scales[:, W : 2 * W], y_grp[1][:])
+        store_words(1, nc.sync)
+        for quad in range(SIDE):
+            eng = nc.sync if quad % 2 else nc.scalar
+            eng.dma_start(
+                out=out_2[:, PACK * quad : PACK * (quad + 1), :].rearrange("s f l -> f s l").bitcast(I32),
+                in_=y_scales[ROWS * quad : ROWS * quad + PACK, :].bitcast(I32).rearrange("f (s w) -> f s w", s=SETS),
+            )

@@ -21,6 +21,7 @@ SIDE = 4
 SETS = 2
 W = 128
 RUN = 4
+ORDER = (0, 2, 1, 3)
 
 
 def tile_rows_pl_kron_gelu_kernel(tc, x, a, bj, hs, b, r, out_0, out_1, out_2):
@@ -67,14 +68,15 @@ def tile_rows_pl_kron_gelu_kernel(tc, x, a, bj, hs, b, r, out_0, out_1, out_2):
         As = [operand("a%d" % s) for s in range(SETS)]
         bs = [operand("b%d" % s) for s in range(SETS)]
         hq = [operand("h%d" % s) for s in range(SETS)]
-        y_raw = [new("y_raw%d" % s, [P, PACK, W], F32) for s in range(SETS)]
+        y_raw = [new("y_raw%d" % s, [P, PACK, W], BF16) for s in range(SETS)]
         y_grp = [new("y_grp%d" % s, [P, W, PACK], BF16) for s in range(SETS)]
         y_codes = [new("y_codes%d" % s, [P, W], U32) for s in range(SETS)]
         y_scales = new("y_scales", [P, SETS * W], U8)
         r_sb = [new("r%d" % s, [P, SIDE, W], F32) for s in range(SETS)]
         act = [new("act%d" % g, [P, W], F32) for g in range(G)]
         h_nat = [new("h_nat%d" % g, [P, W], BF16) for g in range(G)]
-        y_nat = [new("y_nat%d" % g, [P, W], F32) for g in range(G)]
+        y_nat = [new("y_nat%d" % g, [P, W], BF16) for g in range(G)]
+        y_out = [new("y_out%d" % s, [P, SIDE, W], F32) for s in range(SETS)]
         banks = [ps.tile([P, 512], F32, name="bank%d" % g) for g in range(G)]
         vec_rows = new("vec_rows", [P, G * ROWS], F32)
         vec_cols = new("vec_cols", [P, G * ROWS], F32)
@@ -88,20 +90,21 @@ def tile_rows_pl_kron_gelu_kernel(tc, x, a, bj, hs, b, r, out_0, out_1, out_2):
         def load_r(s):
             nc.sync.dma_start(out=r_sb[s][:], in_=r[SIDE * s : SIDE * (s + 1)].rearrange("c k l -> k c l"))
 
-        nc.gpsimd.memset(vec_rows[:], 0.0)
-        for s in range(SETS):
-            nc.sync.dma_start(out=xs[s]["raw"][:], in_=packed_rows(x, s))
-            nc.sync.dma_start(out=As[s]["raw"][:], in_=packed_rows(a, s))
+        nc.vector.memset(vec_rows[:], 0.0)
+        nc.sync.dma_start(out=xs[0]["raw"][:], in_=packed_rows(x, 0))
         for row, v in enumerate((bj, hs)):
-            nc.scalar.dma_start(
+            nc.sync.dma_start(
                 out=vec_rows[row:P:ROWS, :].rearrange("q (g i) -> q g i", i=ROWS),
                 in_=v.rearrange("g (q i) o -> q g (i o)", i=ROWS),
             )
+        nc.sync.dma_start(out=As[0]["raw"][:], in_=packed_rows(a, 0))
+        nc.sync.dma_start(out=xs[1]["raw"][:], in_=packed_rows(x, 1))
+        nc.sync.dma_start(out=As[1]["raw"][:], in_=packed_rows(a, 1))
         for s in range(SETS):
             nc.sync.dma_start(out=bs[s]["raw"][:], in_=packed_rows(b, s))
 
         def first_products(s):
-            for c in range(SIDE):
+            for c in ORDER:
                 product(banks[SIDE * s + c][:, 0:W], c, xs[s]["codes"], xs[s]["scales"], As[s]["codes"], As[s]["scales"])
 
         def gelu(g):
@@ -117,12 +120,24 @@ def tile_rows_pl_kron_gelu_kernel(tc, x, a, bj, hs, b, r, out_0, out_1, out_2):
             nc.sync.dma_start(out=dst[ROWS * c : ROWS * (c + 1), :, :], in_=src[:])
 
         def second_products(s):
-            for c in range(SIDE):
+            for c in ORDER:
                 product(banks[SIDE * s + c][:, W : 2 * W], c, hq[s]["codes"], hq[s]["scales"], bs[s]["codes"], bs[s]["scales"])
 
         def add(g):
             nc.vector.tensor_tensor(out=y_nat[g][:], in0=banks[g][:, W : 2 * W], in1=r_sb[g // SIDE][:, g % SIDE, :], op=ALU.add)
             move(y_raw[g // SIDE], y_nat[g], g)
+
+        def add_f32(g):
+            nc.vector.tensor_tensor(out=y_out[g // SIDE][:, g % SIDE, :], in0=banks[g][:, W : 2 * W], in1=r_sb[g // SIDE][:, g % SIDE, :], op=ALU.add)
+
+        def store_y(s):
+            nc.sync.dma_start(out=out_0[512 * s : 512 * (s + 1), :].rearrange("(c k) l -> k c l", c=SIDE), in_=y_out[s][:])
+
+        def store_words(s):
+            nc.sync.dma_start(out=out_1[s].rearrange("p l u -> p (l u)").bitcast(I32), in_=y_codes[s][:].bitcast(I32))
+
+        def members(s):
+            return [SIDE * s + c for c in ORDER]
 
         iq(xs[0])
         nc.vector.transpose(out=vec_cols[:], in_=vec_rows[:])
@@ -136,43 +151,35 @@ def tile_rows_pl_kron_gelu_kernel(tc, x, a, bj, hs, b, r, out_0, out_1, out_2):
         q(As[1])
         first_products(1)
         load_r(0)
-        for g in range(4):
-            gelu(g)
-            scale(g)
-            move(hq[0]["raw"], h_nat[g], g)
-        iq(bs[0])
-        for g in range(4, 8):
-            gelu(g)
-            scale(g)
-            move(hq[1]["raw"], h_nat[g], g)
+        for s in range(SETS):
+            for g in members(s):
+                gelu(g)
+                scale(g)
+                move(hq[s]["raw"], h_nat[g], g)
         load_r(1)
-        iq(bs[1])
+        iq(bs[0], nc.scalar.copy)
+        iq(bs[1], nc.scalar.copy)
         q(bs[0])
         iq(hq[0])
         q(bs[1])
         q(hq[0])
         second_products(0)
         iq(hq[1])
-        add(0)
         q(hq[1])
         second_products(1)
-        for g in range(1, 8):
-            add(g)
-
-        def store_y(s, eng):
-            eng.dma_start(out=out_0[512 * s : 512 * (s + 1), :].rearrange("(p t) l -> p t l", t=PACK), in_=y_raw[s][:])
-
-        def store_words(s, eng):
-            eng.dma_start(out=out_1[s].rearrange("p l u -> p (l u)").bitcast(I32), in_=y_codes[s][:].bitcast(I32))
-
-        store_y(0, nc.scalar)
-        interleave(nc.vector.tensor_copy, y_grp[0][:], y_raw[0][:])
+        for s in range(SETS):
+            for g in members(s):
+                add(g)
+        for s in range(SETS):
+            for g in members(s):
+                add_f32(g)
+            store_y(s)
+        interleave(nc.scalar.copy, y_grp[0][:], y_raw[0][:])
         quantize(y_codes[0][:], y_scales[:, 0:W], y_grp[0][:])
-        store_words(0, nc.sync)
-        store_y(1, nc.scalar)
+        store_words(0)
         interleave(nc.vector.tensor_copy, y_grp[1][:], y_raw[1][:])
         quantize(y_codes[1][:], y_scales[:, W : 2 * W], y_grp[1][:])
-        store_words(1, nc.sync)
+        store_words(1)
         for quad in range(SIDE):
             eng = nc.sync if quad % 2 else nc.scalar
             eng.dma_start(

@@ -15,12 +15,15 @@ ACT = mybir.ActivationFunctionType
 ALU = mybir.AluOpType
 
 P = 128
-PACK = 4
-ROWS = 32
-SIDE = 4
-SETS = 2
 W = 128
+PACK = 4
+ROWS = W // PACK
+SIDE = P // ROWS
+SETS = G // SIDE
+BANK = 512
+SCALE_ROWS = 4
 RUN = 4
+VECTOR_COLUMNS = 88
 ORDER = (0, 2, 1, 3)
 
 
@@ -34,155 +37,156 @@ def tile_rows_pl_kron_gelu_kernel(tc, x, a, bj, hs, b, r, out_0, out_1, out_2):
         def new(name, shape, dtype):
             return sb.tile(shape, dtype, name=name, align_bytes=64)
 
-        def packed_rows(t, s):
-            return t[SIDE * s : SIDE * (s + 1)].rearrange("c (p j) n -> (c p) j n", j=PACK)
-
-        def interleave(copy, dst, src):
-            copy(
-                out=dst.rearrange("p (c i) t -> p c t i", i=RUN),
-                in_=src.rearrange("p t (c i) -> p c t i", i=RUN),
-            )
-
-        def quantize(codes, scales, grouped):
-            nc.vector.quantize_mx(
-                out=codes.bitcast(FP8X4), scales=scales, in_=grouped.rearrange("p n t -> p (n t)")
-            )
-
-        def product(acc, c, lc, ls, rc, rs):
-            rows = slice(ROWS * c, ROWS * (c + 1))
-            nc.tensor.matmul_mx(
-                out=acc, lhsT=lc[rows, :].bitcast(FP8X4), lhsT_scale=ls[rows, :],
-                rhs=rc[rows, :].bitcast(FP8X4), rhs_scale=rs[rows, :], start=True, stop=True,
-            )
-
-        def operand(name):
-            raw_dt = BF16 if name[0] == "h" else F32
+        def operand(name, packed_dtype):
             return {
-                "raw": new(name + "_raw", [P, PACK, W], raw_dt),
-                "grp": new(name + "_grp", [P, W, PACK], BF16),
+                "packed": new(name + "_packed", [P, PACK, W], packed_dtype),
+                "grouped": new(name + "_grouped", [P, W, PACK], BF16),
                 "codes": new(name + "_codes", [P, W], U32),
                 "scales": new(name + "_scales", [P, W], U8),
             }
 
-        xs = [operand("x%d" % s) for s in range(SETS)]
-        As = [operand("a%d" % s) for s in range(SETS)]
-        bs = [operand("b%d" % s) for s in range(SETS)]
-        hq = [operand("h%d" % s) for s in range(SETS)]
-        y_raw = [new("y_raw%d" % s, [P, PACK, W], BF16) for s in range(SETS)]
-        y_grp = [new("y_grp%d" % s, [P, W, PACK], BF16) for s in range(SETS)]
+        x_op = [operand("x%d" % s, F32) for s in range(SETS)]
+        a_op = [operand("a%d" % s, F32) for s in range(SETS)]
+        b_op = [operand("b%d" % s, F32) for s in range(SETS)]
+        h_op = [operand("h%d" % s, BF16) for s in range(SETS)]
+        y_packed = [new("y_packed%d" % s, [P, PACK, W], BF16) for s in range(SETS)]
+        y_grouped = [new("y_grouped%d" % s, [P, W, PACK], BF16) for s in range(SETS)]
         y_codes = [new("y_codes%d" % s, [P, W], U32) for s in range(SETS)]
         y_scales = new("y_scales", [P, SETS * W], U8)
-        r_sb = [new("r%d" % s, [P, SIDE, W], F32) for s in range(SETS)]
-        act = [new("act%d" % g, [P, W], F32) for g in range(G)]
-        h_nat = [new("h_nat%d" % g, [P, W], BF16) for g in range(G)]
-        y_nat = [new("y_nat%d" % g, [P, W], BF16) for g in range(G)]
-        y_out = [new("y_out%d" % s, [P, SIDE, W], F32) for s in range(SETS)]
-        banks = [ps.tile([P, 512], F32, name="bank%d" % g) for g in range(G)]
+        r_natural = [new("r_natural%d" % s, [P, SIDE, W], F32) for s in range(SETS)]
+        gelu_out = [new("gelu_out%d" % g, [P, W], F32) for g in range(G)]
+        h_natural = [new("h_natural%d" % g, [P, W], BF16) for g in range(G)]
+        y_rounded = [new("y_rounded%d" % g, [P, W], BF16) for g in range(G)]
+        y_natural = [new("y_natural%d" % s, [P, SIDE, W], F32) for s in range(SETS)]
+        banks = [ps.tile([P, BANK], F32, name="bank%d" % g) for g in range(G)]
         vec_rows = new("vec_rows", [P, G * ROWS], F32)
         vec_cols = new("vec_cols", [P, G * ROWS], F32)
-
-        def iq(op, copy=nc.vector.tensor_copy):
-            interleave(copy, op["grp"][:], op["raw"][:])
-
-        def q(op):
-            quantize(op["codes"][:], op["scales"][:], op["grp"][:])
-
-        def load_r(s):
-            nc.sync.dma_start(out=r_sb[s][:], in_=r[SIDE * s : SIDE * (s + 1)].rearrange("c k l -> k c l"))
-
-        nc.vector.memset(vec_rows[:], 0.0)
-        nc.sync.dma_start(out=xs[0]["raw"][:], in_=packed_rows(x, 0))
-        for row, v in enumerate((bj, hs)):
-            nc.sync.dma_start(
-                out=vec_rows[row:P:ROWS, :].rearrange("q (g i) -> q g i", i=ROWS),
-                in_=v.rearrange("g (q i) o -> q g (i o)", i=ROWS),
-            )
-        nc.sync.dma_start(out=As[0]["raw"][:], in_=packed_rows(a, 0))
-        nc.sync.dma_start(out=xs[1]["raw"][:], in_=packed_rows(x, 1))
-        nc.sync.dma_start(out=As[1]["raw"][:], in_=packed_rows(a, 1))
-        for s in range(SETS):
-            nc.sync.dma_start(out=bs[s]["raw"][:], in_=packed_rows(b, s))
-
-        def first_products(s):
-            for c in ORDER:
-                product(banks[SIDE * s + c][:, 0:W], c, xs[s]["codes"], xs[s]["scales"], As[s]["codes"], As[s]["scales"])
-
-        def gelu(g):
-            nc.scalar.activation(out=act[g][:], in_=banks[g][:, 0:W], func=ACT.Gelu_apprx_tanh,
-                                 bias=vec_cols[:, ROWS * g : ROWS * g + 1])
-
-        def scale(g):
-            nc.vector.tensor_scalar(out=h_nat[g][:], in0=act[g][:], scalar1=vec_cols[:, ROWS * g + 1 : ROWS * g + 2],
-                                    scalar2=None, op0=ALU.mult)
-
-        def move(dst, src, g):
-            c = g % SIDE
-            nc.sync.dma_start(out=dst[ROWS * c : ROWS * (c + 1), :, :], in_=src[:])
-
-        def second_products(s):
-            for c in ORDER:
-                product(banks[SIDE * s + c][:, W : 2 * W], c, hq[s]["codes"], hq[s]["scales"], bs[s]["codes"], bs[s]["scales"])
-
-        def add(g):
-            nc.vector.tensor_tensor(out=y_nat[g][:], in0=banks[g][:, W : 2 * W], in1=r_sb[g // SIDE][:, g % SIDE, :], op=ALU.add)
-            move(y_raw[g // SIDE], y_nat[g], g)
-
-        def add_f32(g):
-            nc.vector.tensor_tensor(out=y_out[g // SIDE][:, g % SIDE, :], in0=banks[g][:, W : 2 * W], in1=r_sb[g // SIDE][:, g % SIDE, :], op=ALU.add)
-
-        def store_y(s):
-            nc.sync.dma_start(out=out_0[512 * s : 512 * (s + 1), :].rearrange("(c k) l -> k c l", c=SIDE), in_=y_out[s][:])
-
-        def store_words(s):
-            nc.sync.dma_start(out=out_1[s].rearrange("p l u -> p (l u)").bitcast(I32), in_=y_codes[s][:].bitcast(I32))
 
         def members(s):
             return [SIDE * s + c for c in ORDER]
 
-        iq(xs[0])
+        def tile_rows(g):
+            c = g % SIDE
+            return slice(ROWS * c, ROWS * (c + 1))
+
+        def load_packed(op, src, s):
+            rows = src[SIDE * s : SIDE * (s + 1)].rearrange("c (p t) n -> (c p) t n", t=PACK)
+            nc.sync.dma_start(out=op[s]["packed"][:], in_=rows)
+
+        def load_r(s):
+            nc.sync.dma_start(out=r_natural[s][:], in_=r[SIDE * s : SIDE * (s + 1)].rearrange("c k l -> k c l"))
+
+        def regroup(copy, grouped, packed):
+            copy(
+                out=grouped.rearrange("p (c i) t -> p c t i", i=RUN),
+                in_=packed.rearrange("p t (c i) -> p c t i", i=RUN),
+            )
+
+        def regroup_on(copy, op):
+            regroup(copy, op["grouped"][:], op["packed"][:])
+
+        def regroup_shared(grouped, packed):
+            regroup(nc.scalar.copy, grouped[:, VECTOR_COLUMNS:, :], packed[:, :, VECTOR_COLUMNS:])
+            regroup(nc.vector.tensor_copy, grouped[:, :VECTOR_COLUMNS, :], packed[:, :, :VECTOR_COLUMNS])
+
+        def quantize(codes, scales, grouped):
+            nc.vector.quantize_mx(out=codes.bitcast(FP8X4), scales=scales, in_=grouped.rearrange("p n t -> p (n t)"))
+
+        def quantize_operand(op):
+            quantize(op["codes"][:], op["scales"][:], op["grouped"][:])
+
+        def products(s, first_column, stationary, moving):
+            for g in members(s):
+                rows = tile_rows(g)
+                nc.tensor.matmul_mx(
+                    out=banks[g][:, first_column : first_column + W],
+                    lhsT=stationary["codes"][rows, :].bitcast(FP8X4),
+                    lhsT_scale=stationary["scales"][rows, :],
+                    rhs=moving["codes"][rows, :].bitcast(FP8X4),
+                    rhs_scale=moving["scales"][rows, :],
+                    start=True,
+                    stop=True,
+                )
+
+        def pack(packed, natural, g):
+            nc.sync.dma_start(out=packed[tile_rows(g), :, :], in_=natural[:])
+
+        def make_h(g):
+            bias = vec_cols[:, ROWS * g : ROWS * g + 1]
+            scale = vec_cols[:, ROWS * g + 1 : ROWS * g + 2]
+            nc.scalar.activation(out=gelu_out[g][:], in_=banks[g][:, 0:W], func=ACT.Gelu_apprx_tanh, bias=bias)
+            nc.vector.tensor_scalar(out=h_natural[g][:], in0=gelu_out[g][:], scalar1=scale, scalar2=None, op0=ALU.mult)
+            pack(h_op[g // SIDE]["packed"], h_natural[g], g)
+
+        def add_residual(out, g):
+            residual = r_natural[g // SIDE][:, g % SIDE, :]
+            nc.vector.tensor_tensor(out=out, in0=banks[g][:, W : 2 * W], in1=residual, op=ALU.add)
+
+        def make_rounded_y(g):
+            add_residual(y_rounded[g][:], g)
+            pack(y_packed[g // SIDE], y_rounded[g], g)
+
+        nc.vector.memset(vec_rows[:], 0.0)
+        load_packed(x_op, x, 0)
+        load_packed(a_op, a, 0)
+        for row, vec in enumerate((bj, hs)):
+            nc.sync.dma_start(
+                out=vec_rows[row:P:ROWS, :].rearrange("q (g i) -> q g i", i=ROWS),
+                in_=vec.rearrange("g (q i) o -> q g (i o)", i=ROWS),
+            )
+        load_packed(x_op, x, 1)
+        load_packed(a_op, a, 1)
+        for s in range(SETS):
+            load_packed(b_op, b, s)
+
+        regroup_on(nc.vector.tensor_copy, x_op[0])
+        quantize_operand(x_op[0])
+        regroup_on(nc.vector.tensor_copy, a_op[0])
         nc.vector.transpose(out=vec_cols[:], in_=vec_rows[:])
-        q(xs[0])
-        iq(As[0])
-        q(As[0])
-        first_products(0)
-        iq(xs[1])
-        q(xs[1])
-        iq(As[1])
-        q(As[1])
-        first_products(1)
+        quantize_operand(a_op[0])
+        products(0, 0, x_op[0], a_op[0])
+        regroup_on(nc.vector.tensor_copy, x_op[1])
+        regroup_on(nc.vector.tensor_copy, a_op[1])
+        quantize_operand(x_op[1])
+        quantize_operand(a_op[1])
+        products(1, 0, x_op[1], a_op[1])
+
         load_r(0)
         for s in range(SETS):
             for g in members(s):
-                gelu(g)
-                scale(g)
-                move(hq[s]["raw"], h_nat[g], g)
+                make_h(g)
         load_r(1)
-        iq(bs[0], nc.scalar.copy)
-        iq(bs[1], nc.scalar.copy)
-        q(bs[0])
-        iq(hq[0])
-        q(bs[1])
-        q(hq[0])
-        second_products(0)
-        iq(hq[1])
-        q(hq[1])
-        second_products(1)
+
+        regroup_on(nc.scalar.copy, b_op[0])
+        regroup_on(nc.vector.tensor_copy, b_op[1])
+        quantize_operand(b_op[0])
+        quantize_operand(b_op[1])
+
+        in_turn = members(0) + members(1)
+        regroup_shared(h_op[0]["grouped"], h_op[0]["packed"])
+        quantize_operand(h_op[0])
+        products(0, W, h_op[0], b_op[0])
+        regroup_shared(h_op[1]["grouped"], h_op[1]["packed"])
+        make_rounded_y(in_turn[0])
+        quantize_operand(h_op[1])
+        products(1, W, h_op[1], b_op[1])
+        for g in in_turn[1:]:
+            make_rounded_y(g)
+
         for s in range(SETS):
             for g in members(s):
-                add(g)
+                add_residual(y_natural[s][:, g % SIDE, :], g)
+            set_rows = out_0[SIDE * W * s : SIDE * W * (s + 1), :]
+            nc.sync.dma_start(out=set_rows.rearrange("(c k) l -> k c l", c=SIDE), in_=y_natural[s][:])
+
         for s in range(SETS):
-            for g in members(s):
-                add_f32(g)
-            store_y(s)
-        interleave(nc.scalar.copy, y_grp[0][:], y_raw[0][:])
-        quantize(y_codes[0][:], y_scales[:, 0:W], y_grp[0][:])
-        store_words(0)
-        interleave(nc.vector.tensor_copy, y_grp[1][:], y_raw[1][:])
-        quantize(y_codes[1][:], y_scales[:, W : 2 * W], y_grp[1][:])
-        store_words(1)
-        for quad in range(SIDE):
-            eng = nc.sync if quad % 2 else nc.scalar
-            eng.dma_start(
-                out=out_2[:, PACK * quad : PACK * (quad + 1), :].rearrange("s f l -> f s l").bitcast(I32),
-                in_=y_scales[ROWS * quad : ROWS * quad + PACK, :].bitcast(I32).rearrange("f (s w) -> f s w", s=SETS),
+            regroup_shared(y_grouped[s], y_packed[s])
+            quantize(y_codes[s][:], y_scales[:, W * s : W * (s + 1)], y_grouped[s][:])
+            nc.sync.dma_start(out=out_1[s].rearrange("p l u -> p (l u)").bitcast(I32), in_=y_codes[s][:].bitcast(I32))
+        for c in range(SIDE):
+            queue = nc.sync if c % 2 else nc.scalar
+            live = y_scales[ROWS * c : ROWS * c + SCALE_ROWS, :]
+            queue.dma_start(
+                out=out_2[:, SCALE_ROWS * c : SCALE_ROWS * (c + 1), :].rearrange("s f l -> f s l").bitcast(I32),
+                in_=live.bitcast(I32).rearrange("f (s w) -> f s w", s=SETS),
             )

from contextlib import ExitStack

import concourse.mybir as mybir

G, D, J, K, L = 8, 128, 128, 128, 128
FLOPS = 2 * G * D * J * K + 2 * G * J * K * L

F32 = mybir.dt.float32
BF16 = mybir.dt.bfloat16
U32 = mybir.dt.uint32
I32 = mybir.dt.int32
U8 = mybir.dt.uint8
FP8X4 = mybir.dt.float8_e4m3fn_x4
ACT = mybir.ActivationFunctionType
ALU = mybir.AluOpType

P = 128
W = 128
PACK = 4
ROWS = W // PACK
SIDE = P // ROWS
SETS = G // SIDE
BANK = 512
SCALE_ROWS = 4
RUN = 4
VECTOR_COLUMNS = 88
ORDER = (0, 2, 1, 3)


def tile_rows_pl_kron_gelu_kernel(tc, x, a, bj, hs, b, r, out_0, out_1, out_2):
    nc = tc.nc
    with ExitStack() as ctx:
        sb = ctx.enter_context(tc.tile_pool(name="sb", bufs=1))
        ps = ctx.enter_context(tc.psum_pool(name="ps", bufs=1))
        ctx.enter_context(tc.manual_schedule())

        def new(name, shape, dtype):
            return sb.tile(shape, dtype, name=name, align_bytes=64)

        def operand(name, packed_dtype):
            return {
                "packed": new(name + "_packed", [P, PACK, W], packed_dtype),
                "grouped": new(name + "_grouped", [P, W, PACK], BF16),
                "codes": new(name + "_codes", [P, W], U32),
                "scales": new(name + "_scales", [P, W], U8),
            }

        x_op = [operand("x%d" % s, F32) for s in range(SETS)]
        a_op = [operand("a%d" % s, F32) for s in range(SETS)]
        b_op = [operand("b%d" % s, F32) for s in range(SETS)]
        h_op = [operand("h%d" % s, BF16) for s in range(SETS)]
        y_packed = [new("y_packed%d" % s, [P, PACK, W], BF16) for s in range(SETS)]
        y_grouped = [new("y_grouped%d" % s, [P, W, PACK], BF16) for s in range(SETS)]
        y_codes = [new("y_codes%d" % s, [P, W], U32) for s in range(SETS)]
        y_scales = new("y_scales", [P, SETS * W], U8)
        r_natural = [new("r_natural%d" % s, [P, SIDE, W], F32) for s in range(SETS)]
        gelu_out = [new("gelu_out%d" % g, [P, W], F32) for g in range(G)]
        h_natural = [new("h_natural%d" % g, [P, W], BF16) for g in range(G)]
        y_rounded = [new("y_rounded%d" % g, [P, W], BF16) for g in range(G)]
        y_natural = [new("y_natural%d" % s, [P, SIDE, W], F32) for s in range(SETS)]
        banks = [ps.tile([P, BANK], F32, name="bank%d" % g) for g in range(G)]
        vec_rows = new("vec_rows", [P, G * ROWS], F32)
        vec_cols = new("vec_cols", [P, G * ROWS], F32)

        def members(s):
            return [SIDE * s + c for c in ORDER]

        def tile_rows(g):
            c = g % SIDE
            return slice(ROWS * c, ROWS * (c + 1))

        def load_packed(op, src, s):
            rows = src[SIDE * s : SIDE * (s + 1)].rearrange("c (p t) n -> (c p) t n", t=PACK)
            nc.sync.dma_start(out=op[s]["packed"][:], in_=rows)

        def load_r(s):
            nc.sync.dma_start(out=r_natural[s][:], in_=r[SIDE * s : SIDE * (s + 1)].rearrange("c k l -> k c l"))

        def regroup(copy, grouped, packed):
            copy(
                out=grouped.rearrange("p (c i) t -> p c t i", i=RUN),
                in_=packed.rearrange("p t (c i) -> p c t i", i=RUN),
            )

        def regroup_on(copy, op):
            regroup(copy, op["grouped"][:], op["packed"][:])

        def regroup_shared(grouped, packed):
            regroup(nc.scalar.copy, grouped[:, VECTOR_COLUMNS:, :], packed[:, :, VECTOR_COLUMNS:])
            regroup(nc.vector.tensor_copy, grouped[:, :VECTOR_COLUMNS, :], packed[:, :, :VECTOR_COLUMNS])

        def quantize(codes, scales, grouped):
            nc.vector.quantize_mx(out=codes.bitcast(FP8X4), scales=scales, in_=grouped.rearrange("p n t -> p (n t)"))

        def quantize_operand(op):
            quantize(op["codes"][:], op["scales"][:], op["grouped"][:])

        def products(s, first_column, stationary, moving):
            for g in members(s):
                rows = tile_rows(g)
                nc.tensor.matmul_mx(
                    out=banks[g][:, first_column : first_column + W],
                    lhsT=stationary["codes"][rows, :].bitcast(FP8X4),
                    lhsT_scale=stationary["scales"][rows, :],
                    rhs=moving["codes"][rows, :].bitcast(FP8X4),
                    rhs_scale=moving["scales"][rows, :],
                    start=True,
                    stop=True,
                )

        def pack(packed, natural, g):
            nc.sync.dma_start(out=packed[tile_rows(g), :, :], in_=natural[:])

        def make_h(g):
            bias = vec_cols[:, ROWS * g : ROWS * g + 1]
            scale = vec_cols[:, ROWS * g + 1 : ROWS * g + 2]
            nc.scalar.activation(out=gelu_out[g][:], in_=banks[g][:, 0:W], func=ACT.Gelu_apprx_tanh, bias=bias)
            nc.vector.tensor_scalar(out=h_natural[g][:], in0=gelu_out[g][:], scalar1=scale, scalar2=None, op0=ALU.mult)
            pack(h_op[g // SIDE]["packed"], h_natural[g], g)

        def add_residual(out, g):
            residual = r_natural[g // SIDE][:, g % SIDE, :]
            nc.vector.tensor_tensor(out=out, in0=banks[g][:, W : 2 * W], in1=residual, op=ALU.add)

        def make_rounded_y(g):
            add_residual(y_rounded[g][:], g)
            pack(y_packed[g // SIDE], y_rounded[g], g)

        nc.vector.memset(vec_rows[:], 0.0)
        load_packed(x_op, x, 0)
        load_packed(a_op, a, 0)
        for row, vec in enumerate((bj, hs)):
            nc.sync.dma_start(
                out=vec_rows[row:P:ROWS, :].rearrange("q (g i) -> q g i", i=ROWS),
                in_=vec.rearrange("g (q i) o -> q g (i o)", i=ROWS),
            )
        load_packed(x_op, x, 1)
        load_packed(a_op, a, 1)
        for s in range(SETS):
            load_packed(b_op, b, s)

        regroup_on(nc.vector.tensor_copy, x_op[0])
        quantize_operand(x_op[0])
        regroup_on(nc.vector.tensor_copy, a_op[0])
        nc.vector.transpose(out=vec_cols[:], in_=vec_rows[:])
        quantize_operand(a_op[0])
        products(0, 0, x_op[0], a_op[0])
        regroup_on(nc.vector.tensor_copy, x_op[1])
        regroup_on(nc.vector.tensor_copy, a_op[1])
        quantize_operand(x_op[1])
        quantize_operand(a_op[1])
        products(1, 0, x_op[1], a_op[1])

        load_r(0)
        for s in range(SETS):
            for g in members(s):
                make_h(g)
        load_r(1)

        regroup_on(nc.scalar.copy, b_op[0])
        regroup_on(nc.vector.tensor_copy, b_op[1])
        quantize_operand(b_op[0])
        quantize_operand(b_op[1])

        in_turn = members(0) + members(1)
        regroup_shared(h_op[0]["grouped"], h_op[0]["packed"])
        quantize_operand(h_op[0])
        products(0, W, h_op[0], b_op[0])
        regroup_shared(h_op[1]["grouped"], h_op[1]["packed"])
        make_rounded_y(in_turn[0])
        quantize_operand(h_op[1])
        products(1, W, h_op[1], b_op[1])
        for g in in_turn[1:]:
            make_rounded_y(g)

        for s in range(SETS):
            for g in members(s):
                add_residual(y_natural[s][:, g % SIDE, :], g)
            set_rows = out_0[SIDE * W * s : SIDE * W * (s + 1), :]
            nc.sync.dma_start(out=set_rows.rearrange("(c k) l -> k c l", c=SIDE), in_=y_natural[s][:])

        for s in range(SETS):
            regroup_shared(y_grouped[s], y_packed[s])
            quantize(y_codes[s][:], y_scales[:, W * s : W * (s + 1)], y_grouped[s][:])
            nc.sync.dma_start(out=out_1[s].rearrange("p l u -> p (l u)").bitcast(I32), in_=y_codes[s][:].bitcast(I32))
        for c in range(SIDE):
            queue = nc.sync if c % 2 else nc.scalar
            live = y_scales[ROWS * c : ROWS * c + SCALE_ROWS, :]
            queue.dma_start(
                out=out_2[:, SCALE_ROWS * c : SCALE_ROWS * (c + 1), :].rearrange("s f l -> f s l").bitcast(I32),
                in_=live.bitcast(I32).rearrange("f (s w) -> f s w", s=SETS),
            )
